import numpy as np, ml_dtypes
CORES = [56,64,184,192,312,320,440,448]
N = 8
TK = 64
def setup_inputs(rng):
    x = rng.standard_normal((N, 128, TK), dtype=np.float32).astype(ml_dtypes.bfloat16); w1 = (rng.standard_normal((N, 128, 128), dtype=np.float32) / 8).astype(ml_dtypes.bfloat16)
    wa = np.concatenate(list(w1.astype(np.float64)), axis=1)
    for r in range(N):
        while True:
            near = (np.abs(wa.T @ x[r].astype(np.float64)) < 2e-4).any(axis=0)
            if not near.any(): break
            x[r][:, near] = rng.standard_normal((128, int(near.sum())), dtype=np.float32).astype(ml_dtypes.bfloat16)
    return {"x": x, "dy": rng.standard_normal((N, 128, TK), dtype=np.float32).astype(ml_dtypes.bfloat16), "w1": w1, "w2t": (rng.standard_normal((N, 128, 128), dtype=np.float32) / 8).astype(ml_dtypes.bfloat16)}
def setup_inputs_big(rng):
    d = setup_inputs(rng)
    for k in ("x", "dy", "w1", "w2t"): d[k] = (d[k].astype(np.float32) * 1024.0).astype(d[k].dtype)
    return d
def setup_inputs_small(rng):
    d = setup_inputs(rng)
    for k in ("x", "dy", "w1", "w2t"): d[k] = (d[k].astype(np.float32) * (1 / 1024.0)).astype(d[k].dtype)
    return d
def setup_inputs_apart(rng):
    d = setup_inputs(rng)
    f = (10.0 ** rng.permutation(np.linspace(-1.5, 1.5, N))).astype(np.float32).reshape(N, 1, 1)
    for k in ("x", "dy", "w1", "w2t"): d[k] = (d[k].astype(np.float32) * f).astype(d[k].dtype)
    return d
def reference(x, dy, w1, w2t):
    X, DY, W1, W2T = x.astype(np.float64), dy.astype(np.float64), w1.astype(np.float64), w2t.astype(np.float64)
    dx = np.zeros((N, 128, TK))
    for r in range(N):
        for j in range(N):
            dx[r] += W1[j] @ ((W1[j].T @ X[r] > 0) * (W2T[j].T @ DY[r]))
    return {"dx": dx.astype(ml_dtypes.bfloat16)}

@@ -1,0 +1,186 @@
+from concourse.bass import DstId, RemoteDMATransfer
+from concourse.mybir import AluOpType, ActivationFunctionType
+
+N = 8
+TK = 64
+D = 128
+WC = 2 * D
+NCORES = 512
+NB = 3
+
+SCRATCH = {
+    "stage": ("dram", [128, WC], "bfloat16"),
+    "wall": ("sbuf", [128, N * WC], "bfloat16"),
+    "xd": ("sbuf", [128, 2 * TK], "bfloat16"),
+    "ident": ("sbuf", [128, D], "bfloat16"),
+    "w1t": ("sbuf", [128, N * D], "bfloat16"),
+    "msk": ("sbuf", [128, N * TK], "bfloat16"),
+    "gg": ("sbuf", [128, N * TK], "bfloat16"),
+    "osb": ("sbuf", [128, TK], "bfloat16"),
+    "acc": ("psum", [128, 512], "float32"),
+}
+for _i in range(NB):
+    SCRATCH["zu%d" % _i] = ("psum", [128, 512], "float32")
+    SCRATCH["wt%d" % _i] = ("psum", [128, 1024], "bfloat16")
+
+SEMAPHORES = (["ld", "lw", "one", "idn", "rin", "sent", "fin", "ov", "st"]
+              + ["arr%d" % k for k in range(N)]
+              + ["%s%d" % (p, i) for p in "ztmr" for i in range(N)])
+
+_CACHE = {}
+
+
+def _bits(mask):
+    return [b for b in range(16) if (mask >> b) & 1]
+
+
+def _mask(bits):
+    m = 0
+    for b in bits:
+        m |= 1 << b
+    return m
+
+
+def _plan(T, topo):
+    if "p" in _CACHE:
+        return _CACHE["p"]
+    ranks = [int(c) for c in T.cores]
+    hosts = sorted({topo.host(c) for c in ranks})
+    calls, arr, order = {}, {c: {} for c in ranks}, {}
+
+    def on_chip(c):
+        return [x for x in range(NCORES) if topo.host(x) == topo.host(c) and topo.chip(x) == topo.chip(c) and x != c]
+
+    def twin(s, h):
+        return [t for t in ranks if topo.host(t) == h and topo.chip(t) == topo.chip(s)][0]
+
+    def other(s, h):
+        return [t for t in ranks if topo.host(t) == h and topo.chip(t) != topo.chip(s)][0]
+
+    def rel(s):
+        h = topo.host(s)
+        hr = [k for k in hosts if k != h and topo.rack(k) == topo.rack(h)][0]
+        hd = [k for k in hosts if k != h and not topo.may_write(s, twin(s, k))][0]
+        hc = [k for k in hosts if k not in (h, hr, hd)][0]
+        return h, hr, hc, hd
+
+    def owners(c):
+        own = [x for x in on_chip(c) if topo.may_write(x, other(c, topo.host(c)))]
+        return [x for x in own if topo.die(x) == topo.die(c)], [x for x in own if topo.die(x) != topo.die(c)]
+
+    fwd = {}
+    for k, s in enumerate(ranks):
+        h, hr, hc, hd = rel(s)
+        near, far = owners(s)
+        la, lb, lc = near[0], near[1], far[0]
+        p = owners(twin(s, hc))[1][1]
+        slot = ("wall", k)
+        sem = "arr%d" % k
+        out = _bits(topo.mask(s, twin(s, hc)))
+        inn = [b for b in _bits(topo.mask(s, la)) if b not in out]
+        calls[s] = [
+            (("ld", 32), [([la, lb, lc], inn, "rin", ("stage",), ("stage",)),
+                          ([p], out[0::2], "rin", ("stage",), ("stage",)),
+                          ([twin(s, hc)], out[1::2], sem, ("stage",), slot)]),
+            (None, [([twin(s, hr)], out, sem, ("stage",), slot)]),
+        ]
+        arr[twin(s, hc)][k] = len(out[1::2])
+        arr[twin(s, hr)][k] = len(out)
+        for relay, n_in, dst in ((la, len(inn), other(s, h)), (lb, len(inn), other(s, hr)),
+                                 (lc, len(inn), other(s, hc)), (p, len(out[0::2]), other(s, hd))):
+            eng = _bits(topo.mask(relay, dst))
+            calls[relay] = [(("rin", n_in), [([dst], eng, sem, ("stage",), slot)])]
+            arr[dst][k] = len(eng)
+        f = twin(s, hc)
+        eng = _bits(topo.mask(f, twin(s, hd)))
+        fwd[f] = ((sem, arr[f][k]), [([twin(s, hd)], eng, sem, slot, slot)])
+        arr[twin(s, hd)][k] = len(eng)
+        order[s] = [ranks.index(c) for c in (s, twin(s, hc), twin(s, hr), twin(s, hd),
+                                             other(s, h), other(s, hr), other(s, hc), other(s, hd))]
+    for f in fwd:
+        calls[f].append(fwd[f])
+    _CACHE["p"] = (calls, arr, order)
+    return _CACHE["p"]
+
+
+def _ap(T, key):
+    if key[0] == "stage":
+        return T.stage[:, :]
+    return T.wall[:, key[1] * WC:(key[1] + 1) * WC]
+
+
+def _remote(g, core, T, topo, calls):
+    total = 0
+    for wait, transfers in calls:
+        if wait is not None:
+            g.wait_ge(T.sem[wait[0]], wait[1])
+        lst = []
+        for dsts, eng, rsem, src, dst in transfers:
+            ids = []
+            for d in dsts:
+                rid, pid = topo.addr(d, core)
+                ids.append(DstId(rid=rid, pnc=pid))
+            lst.append(RemoteDMATransfer(dst_ids=ids, dma_engine_mask=_mask(eng), remote_sem=T.sem[rsem],
+                                         srcs=[_ap(T, src)], dsts=[_ap(T, dst) for _ in dsts]))
+            total += len(eng)
+        g.remote_dma_fused(lst, local_sem=T.sem.sent)
+    g.wait_ge(T.sem.sent, total)
+
+
+def rank_program(g, core, T, topo):
+    calls, arr, order = _plan(T, topo)
+    rank = T.rank_of(core)
+    if rank is None:
+        if core in calls:
+            _remote(g, core, T, topo, calls[core])
+        return
+
+    S = T.sem
+    own = rank * WC
+    g.sync.dma_start(T.stage[:, 0:D], T.w1[:, :]).then_inc(S.ld, 16)
+    g.scalar.dma_start(T.stage[:, D:WC], T.w2t[:, :]).then_inc(S.ld, 16)
+    g.sync.dma_start(T.wall[:, own:own + D], T.w1[:, :]).then_inc(S.lw, 16)
+    g.scalar.dma_start(T.wall[:, own + D:own + WC], T.w2t[:, :]).then_inc(S.lw, 16)
+    g.sync.dma_start(T.xd[:, 0:TK], T.x[:, :]).then_inc(S.lw, 16)
+    g.scalar.dma_start(T.xd[:, TK:2 * TK], T.dy[:, :]).then_inc(S.lw, 16)
+
+    g.vector.memset(T.ident[:, :], 1.0).then_inc(S.one, 1)
+    g.wait_ge(S.one, 1)
+    g.affine_select(T.ident[:, :], T.ident[:, :], [[-1, D]], AluOpType.is_equal, 0.0, 0, 1).then_inc(S.idn, 1)
+
+    _remote(g, core, T, topo, calls[core])
+
+    te, ve, se = g.tensor, g.vector, g.scalar
+    x, dy = T.xd[:, 0:TK], T.xd[:, TK:2 * TK]
+
+    def fold(i):
+        te.wait_ge(S["r%d" % i], 2)
+        te.matmul(T.acc[:, 0:TK], T.w1t[:, i * D:(i + 1) * D], T.gg[:, i * TK:(i + 1) * TK],
+                  i == 0, i == N - 1).then_inc(S.fin, 1)
+
+    te.wait_ge(S.lw, 64)
+    te.wait_ge(S.idn, 1)
+    for i, k in enumerate(order[core]):
+        zu, wt = T["zu%d" % (i % NB)], T["wt%d" % (i % NB)]
+        w1, w2t = T.wall[:, k * WC:k * WC + D], T.wall[:, k * WC + D:(k + 1) * WC]
+        if k != rank:
+            te.wait_ge(S["arr%d" % k], arr[core][k])
+        te.matmul(zu[:, 0:TK], w1, x, True, True).then_inc(S["z%d" % i], 1)
+        te.matmul(zu[:, TK:2 * TK], w2t, dy, True, True).then_inc(S["z%d" % i], 1)
+        te.transpose(wt[:, 0:D], w1, T.ident[:, :]).then_inc(S["t%d" % i], 1)
+        if i > 0:
+            fold(i - 1)
+        m, gi = T.msk[:, i * TK:(i + 1) * TK], T.gg[:, i * TK:(i + 1) * TK]
+        ve.wait_ge(S["z%d" % i], 2)
+        ve.tensor_scalar(m, zu[:, 0:TK], 0.0, None, AluOpType.is_gt).then_inc(S["m%d" % i], 1)
+        ve.wait_ge(S["m%d" % i], 1)
+        ve.tensor_tensor(gi, m, zu[:, TK:2 * TK], AluOpType.mult).then_inc(S["r%d" % i], 1)
+        se.wait_ge(S["t%d" % i], 1)
+        se.activation(T.w1t[:, i * D:(i + 1) * D], wt[:, 0:D], ActivationFunctionType.Copy).then_inc(S["r%d" % i], 1)
+    fold(N - 1)
+
+    ve.wait_ge(S.fin, N)
+    ve.tensor_copy(T.osb[:, :], T.acc[:, 0:TK]).then_inc(S.ov, 1)
+    g.sync.wait_ge(S.ov, 1)
+    g.sync.dma_start(T.dx[:, :], T.osb[:, :]).then_inc(S.st, 16)
+    g.sync.wait_ge(S.st, 16)

@@ -6,7 +6,7 @@ TK = 64
 D = 128
 WC = 2 * D
 NCORES = 512
-NB = 3
+NG = 4
 
 SCRATCH = {
     "stage": ("dram", [128, WC], "bfloat16"),
@@ -19,13 +19,14 @@ SCRATCH = {
     "osb": ("sbuf", [128, TK], "bfloat16"),
     "acc": ("psum", [128, 512], "float32"),
 }
-for _i in range(NB):
-    SCRATCH["zu%d" % _i] = ("psum", [128, 512], "float32")
-    SCRATCH["wt%d" % _i] = ("psum", [128, 1024], "bfloat16")
+for _i in range(2):
+    SCRATCH["zb%d" % _i] = ("psum", [128, 512], "float32")
+    SCRATCH["ub%d" % _i] = ("psum", [128, 512], "float32")
+    SCRATCH["wb%d" % _i] = ("psum", [128, 1024], "bfloat16")
 
 SEMAPHORES = (["ld", "lw", "one", "idn", "rin", "sent", "fin", "ov", "st"]
               + ["arr%d" % k for k in range(N)]
-              + ["%s%d" % (p, i) for p in "ztmr" for i in range(N)])
+              + ["%s%d" % (p, i) for p in ("zs", "us", "ts", "ms", "gs", "ws") for i in range(NG)])
 
 _CACHE = {}
 
@@ -46,7 +47,7 @@ def _plan(T, topo):
         return _CACHE["p"]
     ranks = [int(c) for c in T.cores]
     hosts = sorted({topo.host(c) for c in ranks})
-    calls, arr, order = {}, {c: {} for c in ranks}, {}
+    calls, arr, groups = {}, {c: {} for c in ranks}, {}
 
     def on_chip(c):
         return [x for x in range(NCORES) if topo.host(x) == topo.host(c) and topo.chip(x) == topo.chip(c) and x != c]
@@ -74,6 +75,7 @@ def _plan(T, topo):
         near, far = owners(s)
         la, lb, lc = near[0], near[1], far[0]
         p = owners(twin(s, hc))[1][1]
+        m = [x for x in on_chip(s) if x not in near + far and topo.die(x) != topo.die(s)][0]
         slot = ("wall", k)
         sem = "arr%d" % k
         out = _bits(topo.mask(s, twin(s, hc)))
@@ -81,13 +83,13 @@ def _plan(T, topo):
         calls[s] = [
             (("ld", 32), [([la, lb, lc], inn, "rin", ("stage",), ("stage",)),
                           ([p], out[0::2], "rin", ("stage",), ("stage",)),
-                          ([twin(s, hc)], out[1::2], sem, ("stage",), slot)]),
-            (None, [([twin(s, hr)], out, sem, ("stage",), slot)]),
+                          ([m], out[1::2], "rin", ("stage",), ("stage",))]),
+            (None, [([twin(s, hc)], out, sem, ("stage",), slot)]),
         ]
-        arr[twin(s, hc)][k] = len(out[1::2])
-        arr[twin(s, hr)][k] = len(out)
+        arr[twin(s, hc)][k] = len(out)
         for relay, n_in, dst in ((la, len(inn), other(s, h)), (lb, len(inn), other(s, hr)),
-                                 (lc, len(inn), other(s, hc)), (p, len(out[0::2]), other(s, hd))):
+                                 (lc, len(inn), other(s, hc)), (p, len(out[0::2]), other(s, hd)),
+                                 (m, len(out[1::2]), twin(s, hr))):
             eng = _bits(topo.mask(relay, dst))
             calls[relay] = [(("rin", n_in), [([dst], eng, sem, ("stage",), slot)])]
             arr[dst][k] = len(eng)
@@ -95,11 +97,12 @@ def _plan(T, topo):
         eng = _bits(topo.mask(f, twin(s, hd)))
         fwd[f] = ((sem, arr[f][k]), [([twin(s, hd)], eng, sem, slot, slot)])
         arr[twin(s, hd)][k] = len(eng)
-        order[s] = [ranks.index(c) for c in (s, twin(s, hc), twin(s, hr), twin(s, hd),
-                                             other(s, h), other(s, hr), other(s, hc), other(s, hd))]
+        groups[s] = [[ranks.index(c) for c in grp] for grp in (
+            (s,), (twin(s, hc),), (twin(s, hr), other(s, h), other(s, hr), other(s, hc)),
+            (twin(s, hd), other(s, hd)))]
     for f in fwd:
         calls[f].append(fwd[f])
-    _CACHE["p"] = (calls, arr, order)
+    _CACHE["p"] = (calls, arr, groups)
     return _CACHE["p"]
 
 
@@ -109,7 +112,7 @@ def _ap(T, key):
     return T.wall[:, key[1] * WC:(key[1] + 1) * WC]
 
 
-def _remote(g, core, T, topo, calls):
+def _issue(g, core, T, topo, calls):
     total = 0
     for wait, transfers in calls:
         if wait is not None:
@@ -124,15 +127,15 @@ def _remote(g, core, T, topo, calls):
                                          srcs=[_ap(T, src)], dsts=[_ap(T, dst) for _ in dsts]))
             total += len(eng)
         g.remote_dma_fused(lst, local_sem=T.sem.sent)
-    g.wait_ge(T.sem.sent, total)
+    return total
 
 
 def rank_program(g, core, T, topo):
-    calls, arr, order = _plan(T, topo)
+    calls, arr, groups = _plan(T, topo)
     rank = T.rank_of(core)
     if rank is None:
         if core in calls:
-            _remote(g, core, T, topo, calls[core])
+            g.wait_ge(T.sem.sent, _issue(g, core, T, topo, calls[core]))
         return
 
     S = T.sem
@@ -143,41 +146,54 @@ def rank_program(g, core, T, topo):
     g.scalar.dma_start(T.wall[:, own + D:own + WC], T.w2t[:, :]).then_inc(S.lw, 16)
     g.sync.dma_start(T.xd[:, 0:TK], T.x[:, :]).then_inc(S.lw, 16)
     g.scalar.dma_start(T.xd[:, TK:2 * TK], T.dy[:, :]).then_inc(S.lw, 16)
-
     g.vector.memset(T.ident[:, :], 1.0).then_inc(S.one, 1)
+
+    total = _issue(g, core, T, topo, calls[core][0:2])
     g.wait_ge(S.one, 1)
     g.affine_select(T.ident[:, :], T.ident[:, :], [[-1, D]], AluOpType.is_equal, 0.0, 0, 1).then_inc(S.idn, 1)
-
-    _remote(g, core, T, topo, calls[core])
+    total += _issue(g, core, T, topo, calls[core][2:])
+    g.wait_ge(S.sent, total)
 
     te, ve, se = g.tensor, g.vector, g.scalar
     x, dy = T.xd[:, 0:TK], T.xd[:, TK:2 * TK]
+    grp = groups[core]
+    first = [sum(len(q) for q in grp[0:i]) for i in range(NG)]
 
-    def fold(i):
-        te.wait_ge(S["r%d" % i], 2)
-        te.matmul(T.acc[:, 0:TK], T.w1t[:, i * D:(i + 1) * D], T.gg[:, i * TK:(i + 1) * TK],
-                  i == 0, i == N - 1).then_inc(S.fin, 1)
+    def front(gi):
+        ks, i0 = grp[gi], first[gi]
+        n = len(ks)
+        zb, ub, wb = T["zb%d" % (gi % 2)], T["ub%d" % (gi % 2)], T["wb%d" % (gi % 2)]
+        for j, k in enumerate(ks):
+            if k != rank:
+                te.wait_ge(S["arr%d" % k], arr[core][k])
+            te.matmul(zb[:, j * TK:(j + 1) * TK], T.wall[:, k * WC:k * WC + D], x, True, True).then_inc(S["zs%d" % gi], 1)
+        for j, k in enumerate(ks):
+            te.matmul(ub[:, j * TK:(j + 1) * TK], T.wall[:, k * WC + D:(k + 1) * WC], dy, True, True).then_inc(S["us%d" % gi], 1)
+        for j, k in enumerate(ks):
+            te.transpose(wb[:, j * D:(j + 1) * D], T.wall[:, k * WC:k * WC + D], T.ident[:, :]).then_inc(S["ts%d" % gi], 1)
+        mk, gi_ap = T.msk[:, i0 * TK:(i0 + n) * TK], T.gg[:, i0 * TK:(i0 + n) * TK]
+        ve.wait_ge(S["zs%d" % gi], n)
+        ve.tensor_scalar(mk, zb[:, 0:n * TK], 0.0, None, AluOpType.is_gt).then_inc(S["ms%d" % gi], 1)
+        ve.wait_ge(S["ms%d" % gi], 1)
+        ve.wait_ge(S["us%d" % gi], n)
+        ve.tensor_tensor(gi_ap, mk, ub[:, 0:n * TK], AluOpType.mult).then_inc(S["gs%d" % gi], 1)
+        se.wait_ge(S["ts%d" % gi], n)
+        se.activation(T.w1t[:, i0 * D:(i0 + n) * D], wb[:, 0:n * D], ActivationFunctionType.Copy).then_inc(S["ws%d" % gi], 1)
+
+    def fold(gi):
+        te.wait_ge(S["gs%d" % gi], 1)
+        te.wait_ge(S["ws%d" % gi], 1)
+        for i in range(first[gi], first[gi] + len(grp[gi])):
+            te.matmul(T.acc[:, 0:TK], T.w1t[:, i * D:(i + 1) * D], T.gg[:, i * TK:(i + 1) * TK],
+                      i == 0, i == N - 1).then_inc(S.fin, 1)
 
     te.wait_ge(S.lw, 64)
     te.wait_ge(S.idn, 1)
-    for i, k in enumerate(order[core]):
-        zu, wt = T["zu%d" % (i % NB)], T["wt%d" % (i % NB)]
-        w1, w2t = T.wall[:, k * WC:k * WC + D], T.wall[:, k * WC + D:(k + 1) * WC]
-        if k != rank:
-            te.wait_ge(S["arr%d" % k], arr[core][k])
-        te.matmul(zu[:, 0:TK], w1, x, True, True).then_inc(S["z%d" % i], 1)
-        te.matmul(zu[:, TK:2 * TK], w2t, dy, True, True).then_inc(S["z%d" % i], 1)
-        te.transpose(wt[:, 0:D], w1, T.ident[:, :]).then_inc(S["t%d" % i], 1)
-        if i > 0:
-            fold(i - 1)
-        m, gi = T.msk[:, i * TK:(i + 1) * TK], T.gg[:, i * TK:(i + 1) * TK]
-        ve.wait_ge(S["z%d" % i], 2)
-        ve.tensor_scalar(m, zu[:, 0:TK], 0.0, None, AluOpType.is_gt).then_inc(S["m%d" % i], 1)
-        ve.wait_ge(S["m%d" % i], 1)
-        ve.tensor_tensor(gi, m, zu[:, TK:2 * TK], AluOpType.mult).then_inc(S["r%d" % i], 1)
-        se.wait_ge(S["t%d" % i], 1)
-        se.activation(T.w1t[:, i * D:(i + 1) * D], wt[:, 0:D], ActivationFunctionType.Copy).then_inc(S["r%d" % i], 1)
-    fold(N - 1)
+    front(0)
+    for gi in range(1, NG):
+        front(gi)
+        fold(gi - 1)
+    fold(NG - 1)
 
     ve.wait_ge(S.fin, N)
     ve.tensor_copy(T.osb[:, :], T.acc[:, 0:TK]).then_inc(S.ov, 1)

@@ -3,29 +3,36 @@ from concourse.mybir import AluOpType, ActivationFunctionType
 
 N = 8
 TK = 64
+T2 = 2 * TK
 D = 128
 WC = 2 * D
 NCORES = 512
-NG = 4
+NG = 3
+NS = 4
 
 SCRATCH = {
-    "stage": ("dram", [128, WC], "bfloat16"),
+    "st0": ("dram", [128, D], "bfloat16"),
+    "st1": ("dram", [128, D], "bfloat16"),
     "wall": ("sbuf", [128, N * WC], "bfloat16"),
-    "xd": ("sbuf", [128, 2 * TK], "bfloat16"),
+    "xo": ("sbuf", [128, T2], "bfloat16"),
+    "xf": ("sbuf", [128, T2], "bfloat16"),
     "ident": ("sbuf", [128, D], "bfloat16"),
-    "w1t": ("sbuf", [128, N * D], "bfloat16"),
-    "msk": ("sbuf", [128, N * TK], "bfloat16"),
-    "gg": ("sbuf", [128, N * TK], "bfloat16"),
+    "w1t": ("sbuf", [128, NS * D], "bfloat16"),
+    "msk": ("sbuf", [128, NS * T2], "bfloat16"),
+    "gg": ("sbuf", [128, NS * T2], "bfloat16"),
+    "pf": ("sbuf", [128, TK], "bfloat16"),
+    "pin": ("sbuf", [128, TK], "bfloat16"),
     "osb": ("sbuf", [128, TK], "bfloat16"),
-    "acc": ("psum", [128, 512], "float32"),
+    "acco": ("psum", [128, 512], "float32"),
+    "accf": ("psum", [128, 512], "float32"),
 }
 for _i in range(2):
     SCRATCH["zb%d" % _i] = ("psum", [128, 512], "float32")
     SCRATCH["ub%d" % _i] = ("psum", [128, 512], "float32")
     SCRATCH["wb%d" % _i] = ("psum", [128, 1024], "bfloat16")
 
-SEMAPHORES = (["ld", "lw", "one", "idn", "rin", "sent", "fin", "ov", "st"]
-              + ["arr%d" % k for k in range(N)]
+SEMAPHORES = (["ld", "lt", "lw", "one", "idn", "rin", "sent", "tarr", "parr", "finf", "fino", "pv", "ov", "st"]
+              + ["a%d_%d" % (hf, k) for hf in range(2) for k in range(N)]
               + ["%s%d" % (p, i) for p in ("zs", "us", "ts", "ms", "gs", "ws") for i in range(NG)])
 
 _CACHE = {}
@@ -47,7 +54,7 @@ def _plan(T, topo):
         return _CACHE["p"]
     ranks = [int(c) for c in T.cores]
     hosts = sorted({topo.host(c) for c in ranks})
-    calls, arr, groups = {}, {c: {} for c in ranks}, {}
+    feeds, relay, arr, peers, groups = {}, {}, {c: {} for c in ranks}, {}, {}
 
     def on_chip(c):
         return [x for x in range(NCORES) if topo.host(x) == topo.host(c) and topo.chip(x) == topo.chip(c) and x != c]
@@ -58,136 +65,122 @@ def _plan(T, topo):
     def other(s, h):
         return [t for t in ranks if topo.host(t) == h and topo.chip(t) != topo.chip(s)][0]
 
-    def rel(s):
-        h = topo.host(s)
-        hr = [k for k in hosts if k != h and topo.rack(k) == topo.rack(h)][0]
-        hd = [k for k in hosts if k != h and not topo.may_write(s, twin(s, k))][0]
-        hc = [k for k in hosts if k not in (h, hr, hd)][0]
-        return h, hr, hc, hd
-
-    def owners(c):
-        own = [x for x in on_chip(c) if topo.may_write(x, other(c, topo.host(c)))]
-        return [x for x in own if topo.die(x) == topo.die(c)], [x for x in own if topo.die(x) != topo.die(c)]
-
-    fwd = {}
     for k, s in enumerate(ranks):
-        h, hr, hc, hd = rel(s)
-        near, far = owners(s)
-        la, lb, lc = near[0], near[1], far[0]
-        p = owners(twin(s, hc))[1][1]
-        m = [x for x in on_chip(s) if x not in near + far and topo.die(x) != topo.die(s)][0]
-        slot = ("wall", k)
-        sem = "arr%d" % k
+        h = topo.host(s)
+        hr = [q for q in hosts if q != h and topo.rack(q) == topo.rack(h)][0]
+        hc = [q for q in hosts if topo.rack(q) != topo.rack(h) and topo.may_write(s, twin(s, q))][0]
+        own = [x for x in on_chip(s) if topo.may_write(x, other(s, h))]
+        dies = ([x for x in own if topo.die(x) == topo.die(s)], [x for x in own if topo.die(x) != topo.die(s)])
         out = _bits(topo.mask(s, twin(s, hc)))
-        inn = [b for b in _bits(topo.mask(s, la)) if b not in out]
-        calls[s] = [
-            (("ld", 32), [([la, lb, lc], inn, "rin", ("stage",), ("stage",)),
-                          ([p], out[0::2], "rin", ("stage",), ("stage",)),
-                          ([m], out[1::2], "rin", ("stage",), ("stage",))]),
-            (None, [([twin(s, hc)], out, sem, ("stage",), slot)]),
-        ]
-        arr[twin(s, hc)][k] = len(out)
-        for relay, n_in, dst in ((la, len(inn), other(s, h)), (lb, len(inn), other(s, hr)),
-                                 (lc, len(inn), other(s, hc)), (p, len(out[0::2]), other(s, hd)),
-                                 (m, len(out[1::2]), twin(s, hr))):
-            eng = _bits(topo.mask(relay, dst))
-            calls[relay] = [(("rin", n_in), [([dst], eng, sem, ("stage",), slot)])]
-            arr[dst][k] = len(eng)
-        f = twin(s, hc)
-        eng = _bits(topo.mask(f, twin(s, hd)))
-        fwd[f] = ((sem, arr[f][k]), [([twin(s, hd)], eng, sem, slot, slot)])
-        arr[twin(s, hd)][k] = len(eng)
-        groups[s] = [[ranks.index(c) for c in grp] for grp in (
-            (s,), (twin(s, hc),), (twin(s, hr), other(s, h), other(s, hr), other(s, hc)),
-            (twin(s, hd), other(s, hd)))]
-    for f in fwd:
-        calls[f].append(fwd[f])
-    _CACHE["p"] = (calls, arr, groups)
+        inn = [b for b in _bits(topo.mask(s, own[0])) if b not in out]
+        feeds[s] = []
+        for hf in range(2):
+            eng_in = inn[1 - hf::2]
+            feeds[s].append((dies[hf][0:2], eng_in, hf))
+            for r, dst in zip(dies[hf][0:2], (other(s, h), other(s, hr))):
+                relay[r] = (hf, len(eng_in), dst, k)
+                arr[dst].setdefault(k, [None, None])[hf] = ("a%d_%d" % (hf, k), len(_bits(topo.mask(r, dst))))
+        arr[twin(s, hr)][k] = [("a0_%d" % k, len(out)), None]
+        peers[s] = (twin(s, hc), twin(s, hr), out)
+        groups[s] = [[ranks.index(c) for c in grp] for grp in ((s,), (twin(s, hr),), (other(s, h), other(s, hr)))]
+    _CACHE["p"] = (feeds, relay, arr, peers, groups)
     return _CACHE["p"]
 
 
-def _ap(T, key):
-    if key[0] == "stage":
-        return T.stage[:, :]
-    return T.wall[:, key[1] * WC:(key[1] + 1) * WC]
-
-
-def _issue(g, core, T, topo, calls):
-    total = 0
-    for wait, transfers in calls:
-        if wait is not None:
-            g.wait_ge(T.sem[wait[0]], wait[1])
-        lst = []
-        for dsts, eng, rsem, src, dst in transfers:
-            ids = []
-            for d in dsts:
-                rid, pid = topo.addr(d, core)
-                ids.append(DstId(rid=rid, pnc=pid))
-            lst.append(RemoteDMATransfer(dst_ids=ids, dma_engine_mask=_mask(eng), remote_sem=T.sem[rsem],
-                                         srcs=[_ap(T, src)], dsts=[_ap(T, dst) for _ in dsts]))
-            total += len(eng)
-        g.remote_dma_fused(lst, local_sem=T.sem.sent)
+def _send(g, core, T, topo, transfers):
+    lst, total = [], 0
+    for dsts, eng, rsem, src, dst in transfers:
+        ids = []
+        for d in dsts:
+            rid, pid = topo.addr(d, core)
+            ids.append(DstId(rid=rid, pnc=pid))
+        lst.append(RemoteDMATransfer(dst_ids=ids, dma_engine_mask=_mask(eng), remote_sem=T.sem[rsem],
+                                     srcs=[src], dsts=[dst for _ in dsts]))
+        total += len(eng)
+    g.remote_dma_fused(lst, local_sem=T.sem.sent)
     return total
 
 
 def rank_program(g, core, T, topo):
-    calls, arr, groups = _plan(T, topo)
+    feeds, relay, arr, peers, groups = _plan(T, topo)
     rank = T.rank_of(core)
+    S = T.sem
     if rank is None:
-        if core in calls:
-            g.wait_ge(T.sem.sent, _issue(g, core, T, topo, calls[core]))
+        if core in relay:
+            hf, n_in, dst, k = relay[core]
+            g.wait_ge(S.rin, n_in)
+            c0 = k * WC + hf * D
+            g.wait_ge(S.sent, _send(g, core, T, topo, [([dst], _bits(topo.mask(core, dst)), "a%d_%d" % (hf, k),
+                                                        T["st%d" % hf][:, :], T.wall[:, c0:c0 + D])]))
         return
 
-    S = T.sem
+    partner, rtwin, out = peers[core]
     own = rank * WC
-    g.sync.dma_start(T.stage[:, 0:D], T.w1[:, :]).then_inc(S.ld, 16)
-    g.scalar.dma_start(T.stage[:, D:WC], T.w2t[:, :]).then_inc(S.ld, 16)
+    g.sync.dma_start(T.st0[:, :], T.w1[:, :]).then_inc(S.ld, 16)
+    g.scalar.dma_start(T.st1[:, :], T.w2t[:, :]).then_inc(S.ld, 16)
+    g.sync.dma_start(T.xo[:, 0:TK], T.x[:, :]).then_inc(S.lt, 16)
+    g.scalar.dma_start(T.xo[:, TK:T2], T.dy[:, :]).then_inc(S.lt, 16)
     g.sync.dma_start(T.wall[:, own:own + D], T.w1[:, :]).then_inc(S.lw, 16)
     g.scalar.dma_start(T.wall[:, own + D:own + WC], T.w2t[:, :]).then_inc(S.lw, 16)
-    g.sync.dma_start(T.xd[:, 0:TK], T.x[:, :]).then_inc(S.lw, 16)
-    g.scalar.dma_start(T.xd[:, TK:2 * TK], T.dy[:, :]).then_inc(S.lw, 16)
     g.vector.memset(T.ident[:, :], 1.0).then_inc(S.one, 1)
 
-    total = _issue(g, core, T, topo, calls[core][0:2])
+    g.wait_ge(S.ld, 32)
+    total = _send(g, core, T, topo, [(dsts, eng, "rin", T["st%d" % hf][:, :], T["st%d" % hf][:, :])
+                                     for dsts, eng, hf in feeds[core]])
+    g.wait_ge(S.lt, 32)
+    total += _send(g, core, T, topo, [([partner], out, "tarr", T.xo[:, :], T.xf[:, :])])
+    g.wait_ge(S.lw, 32)
+    total += _send(g, core, T, topo, [([rtwin], out, "a0_%d" % rank, T.wall[:, own:own + WC], T.wall[:, own:own + WC])])
     g.wait_ge(S.one, 1)
     g.affine_select(T.ident[:, :], T.ident[:, :], [[-1, D]], AluOpType.is_equal, 0.0, 0, 1).then_inc(S.idn, 1)
-    total += _issue(g, core, T, topo, calls[core][2:])
+    g.wait_ge(S.pv, 1)
+    total += _send(g, core, T, topo, [([partner], out, "parr", T.pf[:, :], T.pin[:, :])])
     g.wait_ge(S.sent, total)
 
     te, ve, se = g.tensor, g.vector, g.scalar
-    x, dy = T.xd[:, 0:TK], T.xd[:, TK:2 * TK]
     grp = groups[core]
     first = [sum(len(q) for q in grp[0:i]) for i in range(NG)]
+
+    def landed(k, hf):
+        if k != rank and arr[core][k][hf] is not None:
+            te.wait_ge(S[arr[core][k][hf][0]], arr[core][k][hf][1])
 
     def front(gi):
         ks, i0 = grp[gi], first[gi]
         n = len(ks)
         zb, ub, wb = T["zb%d" % (gi % 2)], T["ub%d" % (gi % 2)], T["wb%d" % (gi % 2)]
         for j, k in enumerate(ks):
-            if k != rank:
-                te.wait_ge(S["arr%d" % k], arr[core][k])
-            te.matmul(zb[:, j * TK:(j + 1) * TK], T.wall[:, k * WC:k * WC + D], x, True, True).then_inc(S["zs%d" % gi], 1)
-        for j, k in enumerate(ks):
-            te.matmul(ub[:, j * TK:(j + 1) * TK], T.wall[:, k * WC + D:(k + 1) * WC], dy, True, True).then_inc(S["us%d" % gi], 1)
+            landed(k, 0)
+            for q, tok in enumerate((T.xo, T.xf)):
+                te.matmul(zb[:, j * T2 + q * TK:j * T2 + (q + 1) * TK], T.wall[:, k * WC:k * WC + D], tok[:, 0:TK],
+                          True, True).then_inc(S["zs%d" % gi], 1)
         for j, k in enumerate(ks):
             te.transpose(wb[:, j * D:(j + 1) * D], T.wall[:, k * WC:k * WC + D], T.ident[:, :]).then_inc(S["ts%d" % gi], 1)
-        mk, gi_ap = T.msk[:, i0 * TK:(i0 + n) * TK], T.gg[:, i0 * TK:(i0 + n) * TK]
-        ve.wait_ge(S["zs%d" % gi], n)
-        ve.tensor_scalar(mk, zb[:, 0:n * TK], 0.0, None, AluOpType.is_gt).then_inc(S["ms%d" % gi], 1)
+        for j, k in enumerate(ks):
+            landed(k, 1)
+            for q, tok in enumerate((T.xo, T.xf)):
+                te.matmul(ub[:, j * T2 + q * TK:j * T2 + (q + 1) * TK], T.wall[:, k * WC + D:(k + 1) * WC], tok[:, TK:T2],
+                          True, True).then_inc(S["us%d" % gi], 1)
+        mk, gi_ap = T.msk[:, i0 * T2:(i0 + n) * T2], T.gg[:, i0 * T2:(i0 + n) * T2]
+        ve.wait_ge(S["zs%d" % gi], 2 * n)
+        ve.tensor_scalar(mk, zb[:, 0:n * T2], 0.0, None, AluOpType.is_gt).then_inc(S["ms%d" % gi], 1)
         ve.wait_ge(S["ms%d" % gi], 1)
-        ve.wait_ge(S["us%d" % gi], n)
-        ve.tensor_tensor(gi_ap, mk, ub[:, 0:n * TK], AluOpType.mult).then_inc(S["gs%d" % gi], 1)
+        ve.wait_ge(S["us%d" % gi], 2 * n)
+        ve.tensor_tensor(gi_ap, mk, ub[:, 0:n * T2], AluOpType.mult).then_inc(S["gs%d" % gi], 1)
         se.wait_ge(S["ts%d" % gi], n)
         se.activation(T.w1t[:, i0 * D:(i0 + n) * D], wb[:, 0:n * D], ActivationFunctionType.Copy).then_inc(S["ws%d" % gi], 1)
 
     def fold(gi):
         te.wait_ge(S["gs%d" % gi], 1)
         te.wait_ge(S["ws%d" % gi], 1)
-        for i in range(first[gi], first[gi] + len(grp[gi])):
-            te.matmul(T.acc[:, 0:TK], T.w1t[:, i * D:(i + 1) * D], T.gg[:, i * TK:(i + 1) * TK],
-                      i == 0, i == N - 1).then_inc(S.fin, 1)
+        for acc, q, sem in ((T.accf, 1, S.finf), (T.acco, 0, S.fino)):
+            for i in range(first[gi], first[gi] + len(grp[gi])):
+                te.matmul(acc[:, 0:TK], T.w1t[:, i * D:(i + 1) * D], T.gg[:, i * T2 + q * TK:i * T2 + (q + 1) * TK],
+                          i == 0, i == NS - 1).then_inc(sem, 1)
 
-    te.wait_ge(S.lw, 64)
+    te.wait_ge(S.lw, 32)
+    te.wait_ge(S.lt, 32)
+    te.wait_ge(S.tarr, len(out))
     te.wait_ge(S.idn, 1)
     front(0)
     for gi in range(1, NG):
@@ -195,8 +188,11 @@ def rank_program(g, core, T, topo):
         fold(gi - 1)
     fold(NG - 1)
 
-    ve.wait_ge(S.fin, N)
-    ve.tensor_copy(T.osb[:, :], T.acc[:, 0:TK]).then_inc(S.ov, 1)
+    ve.wait_ge(S.finf, NS)
+    ve.tensor_copy(T.pf[:, :], T.accf[:, 0:TK]).then_inc(S.pv, 1)
+    ve.wait_ge(S.fino, NS)
+    ve.wait_ge(S.parr, len(out))
+    ve.tensor_tensor(T.osb[:, :], T.acco[:, 0:TK], T.pin[:, :], AluOpType.add).then_inc(S.ov, 1)
     g.sync.wait_ge(S.ov, 1)
     g.sync.dma_start(T.dx[:, :], T.osb[:, :]).then_inc(S.st, 16)
     g.sync.wait_ge(S.st, 16)

from concourse.bass import DstId, RemoteDMATransfer
from concourse.mybir import AluOpType, ActivationFunctionType

N = 8
TK = 64
T2 = 2 * TK
D = 128
WC = 2 * D
NCORES = 512
NG = 3
NS = 4

SCRATCH = {
    "st0": ("dram", [128, D], "bfloat16"),
    "st1": ("dram", [128, D], "bfloat16"),
    "wall": ("sbuf", [128, N * WC], "bfloat16"),
    "xo": ("sbuf", [128, T2], "bfloat16"),
    "xf": ("sbuf", [128, T2], "bfloat16"),
    "ident": ("sbuf", [128, D], "bfloat16"),
    "w1t": ("sbuf", [128, NS * D], "bfloat16"),
    "msk": ("sbuf", [128, NS * T2], "bfloat16"),
    "gg": ("sbuf", [128, NS * T2], "bfloat16"),
    "pf": ("sbuf", [128, TK], "bfloat16"),
    "pin": ("sbuf", [128, TK], "bfloat16"),
    "osb": ("sbuf", [128, TK], "bfloat16"),
    "acco": ("psum", [128, 512], "float32"),
    "accf": ("psum", [128, 512], "float32"),
}
for _i in range(2):
    SCRATCH["zb%d" % _i] = ("psum", [128, 512], "float32")
    SCRATCH["ub%d" % _i] = ("psum", [128, 512], "float32")
    SCRATCH["wb%d" % _i] = ("psum", [128, 1024], "bfloat16")

SEMAPHORES = (["ld", "lt", "lw", "one", "idn", "rin", "sent", "tarr", "parr", "finf", "fino", "pv", "ov", "st"]
              + ["a%d_%d" % (hf, k) for hf in range(2) for k in range(N)]
              + ["%s%d" % (p, i) for p in ("zs", "us", "ts", "ms", "gs", "ws") for i in range(NG)])

_CACHE = {}


def _bits(mask):
    return [b for b in range(16) if (mask >> b) & 1]


def _mask(bits):
    m = 0
    for b in bits:
        m |= 1 << b
    return m


def _plan(T, topo):
    if "p" in _CACHE:
        return _CACHE["p"]
    ranks = [int(c) for c in T.cores]
    hosts = sorted({topo.host(c) for c in ranks})
    feeds, relay, arr, peers, groups = {}, {}, {c: {} for c in ranks}, {}, {}

    def on_chip(c):
        return [x for x in range(NCORES) if topo.host(x) == topo.host(c) and topo.chip(x) == topo.chip(c) and x != c]

    def twin(s, h):
        return [t for t in ranks if topo.host(t) == h and topo.chip(t) == topo.chip(s)][0]

    def other(s, h):
        return [t for t in ranks if topo.host(t) == h and topo.chip(t) != topo.chip(s)][0]

    for k, s in enumerate(ranks):
        h = topo.host(s)
        hr = [q for q in hosts if q != h and topo.rack(q) == topo.rack(h)][0]
        hc = [q for q in hosts if topo.rack(q) != topo.rack(h) and topo.may_write(s, twin(s, q))][0]
        own = [x for x in on_chip(s) if topo.may_write(x, other(s, h))]
        dies = ([x for x in own if topo.die(x) == topo.die(s)], [x for x in own if topo.die(x) != topo.die(s)])
        out = _bits(topo.mask(s, twin(s, hc)))
        inn = [b for b in _bits(topo.mask(s, own[0])) if b not in out]
        feeds[s] = []
        for hf in range(2):
            eng_in = inn[1 - hf::2]
            feeds[s].append((dies[hf][0:2], eng_in, hf))
            for r, dst in zip(dies[hf][0:2], (other(s, h), other(s, hr))):
                relay[r] = (hf, len(eng_in), dst, k)
                arr[dst].setdefault(k, [None, None])[hf] = ("a%d_%d" % (hf, k), len(_bits(topo.mask(r, dst))))
        arr[twin(s, hr)][k] = [("a0_%d" % k, len(out)), None]
        peers[s] = (twin(s, hc), twin(s, hr), out)
        groups[s] = [[ranks.index(c) for c in grp] for grp in ((s,), (twin(s, hr),), (other(s, h), other(s, hr)))]
    _CACHE["p"] = (feeds, relay, arr, peers, groups)
    return _CACHE["p"]


def _send(g, core, T, topo, transfers):
    lst, total = [], 0
    for dsts, eng, rsem, src, dst in transfers:
        ids = []
        for d in dsts:
            rid, pid = topo.addr(d, core)
            ids.append(DstId(rid=rid, pnc=pid))
        lst.append(RemoteDMATransfer(dst_ids=ids, dma_engine_mask=_mask(eng), remote_sem=T.sem[rsem],
                                     srcs=[src], dsts=[dst for _ in dsts]))
        total += len(eng)
    g.remote_dma_fused(lst, local_sem=T.sem.sent)
    return total


def rank_program(g, core, T, topo):
    feeds, relay, arr, peers, groups = _plan(T, topo)
    rank = T.rank_of(core)
    S = T.sem
    if rank is None:
        if core in relay:
            hf, n_in, dst, k = relay[core]
            g.wait_ge(S.rin, n_in)
            c0 = k * WC + hf * D
            g.wait_ge(S.sent, _send(g, core, T, topo, [([dst], _bits(topo.mask(core, dst)), "a%d_%d" % (hf, k),
                                                        T["st%d" % hf][:, :], T.wall[:, c0:c0 + D])]))
        return

    partner, rtwin, out = peers[core]
    own = rank * WC
    g.sync.dma_start(T.st0[:, :], T.w1[:, :]).then_inc(S.ld, 16)
    g.scalar.dma_start(T.st1[:, :], T.w2t[:, :]).then_inc(S.ld, 16)
    g.sync.dma_start(T.xo[:, 0:TK], T.x[:, :]).then_inc(S.lt, 16)
    g.scalar.dma_start(T.xo[:, TK:T2], T.dy[:, :]).then_inc(S.lt, 16)
    g.sync.dma_start(T.wall[:, own:own + D], T.w1[:, :]).then_inc(S.lw, 16)
    g.scalar.dma_start(T.wall[:, own + D:own + WC], T.w2t[:, :]).then_inc(S.lw, 16)
    g.vector.memset(T.ident[:, :], 1.0).then_inc(S.one, 1)

    g.wait_ge(S.ld, 32)
    total = _send(g, core, T, topo, [(dsts, eng, "rin", T["st%d" % hf][:, :], T["st%d" % hf][:, :])
                                     for dsts, eng, hf in feeds[core]])
    g.wait_ge(S.lt, 32)
    total += _send(g, core, T, topo, [([partner], out, "tarr", T.xo[:, :], T.xf[:, :])])
    g.wait_ge(S.lw, 32)
    total += _send(g, core, T, topo, [([rtwin], out, "a0_%d" % rank, T.wall[:, own:own + WC], T.wall[:, own:own + WC])])
    g.wait_ge(S.one, 1)
    g.affine_select(T.ident[:, :], T.ident[:, :], [[-1, D]], AluOpType.is_equal, 0.0, 0, 1).then_inc(S.idn, 1)
    g.wait_ge(S.pv, 1)
    total += _send(g, core, T, topo, [([partner], out, "parr", T.pf[:, :], T.pin[:, :])])
    g.wait_ge(S.sent, total)

    te, ve, se = g.tensor, g.vector, g.scalar
    grp = groups[core]
    first = [sum(len(q) for q in grp[0:i]) for i in range(NG)]

    def landed(k, hf):
        if k != rank and arr[core][k][hf] is not None:
            te.wait_ge(S[arr[core][k][hf][0]], arr[core][k][hf][1])

    def front(gi):
        ks, i0 = grp[gi], first[gi]
        n = len(ks)
        zb, ub, wb = T["zb%d" % (gi % 2)], T["ub%d" % (gi % 2)], T["wb%d" % (gi % 2)]
        for j, k in enumerate(ks):
            landed(k, 0)
            for q, tok in enumerate((T.xo, T.xf)):
                te.matmul(zb[:, j * T2 + q * TK:j * T2 + (q + 1) * TK], T.wall[:, k * WC:k * WC + D], tok[:, 0:TK],
                          True, True).then_inc(S["zs%d" % gi], 1)
        for j, k in enumerate(ks):
            te.transpose(wb[:, j * D:(j + 1) * D], T.wall[:, k * WC:k * WC + D], T.ident[:, :]).then_inc(S["ts%d" % gi], 1)
        for j, k in enumerate(ks):
            landed(k, 1)
            for q, tok in enumerate((T.xo, T.xf)):
                te.matmul(ub[:, j * T2 + q * TK:j * T2 + (q + 1) * TK], T.wall[:, k * WC + D:(k + 1) * WC], tok[:, TK:T2],
                          True, True).then_inc(S["us%d" % gi], 1)
        mk, gi_ap = T.msk[:, i0 * T2:(i0 + n) * T2], T.gg[:, i0 * T2:(i0 + n) * T2]
        ve.wait_ge(S["zs%d" % gi], 2 * n)
        ve.tensor_scalar(mk, zb[:, 0:n * T2], 0.0, None, AluOpType.is_gt).then_inc(S["ms%d" % gi], 1)
        ve.wait_ge(S["ms%d" % gi], 1)
        ve.wait_ge(S["us%d" % gi], 2 * n)
        ve.tensor_tensor(gi_ap, mk, ub[:, 0:n * T2], AluOpType.mult).then_inc(S["gs%d" % gi], 1)
        se.wait_ge(S["ts%d" % gi], n)
        se.activation(T.w1t[:, i0 * D:(i0 + n) * D], wb[:, 0:n * D], ActivationFunctionType.Copy).then_inc(S["ws%d" % gi], 1)

    def fold(gi):
        te.wait_ge(S["gs%d" % gi], 1)
        te.wait_ge(S["ws%d" % gi], 1)
        for acc, q, sem in ((T.accf, 1, S.finf), (T.acco, 0, S.fino)):
            for i in range(first[gi], first[gi] + len(grp[gi])):
                te.matmul(acc[:, 0:TK], T.w1t[:, i * D:(i + 1) * D], T.gg[:, i * T2 + q * TK:i * T2 + (q + 1) * TK],
                          i == 0, i == NS - 1).then_inc(sem, 1)

    te.wait_ge(S.lw, 32)
    te.wait_ge(S.lt, 32)
    te.wait_ge(S.tarr, len(out))
    te.wait_ge(S.idn, 1)
    front(0)
    for gi in range(1, NG):
        front(gi)
        fold(gi - 1)
    fold(NG - 1)

    ve.wait_ge(S.finf, NS)
    ve.tensor_copy(T.pf[:, :], T.accf[:, 0:TK]).then_inc(S.pv, 1)
    ve.wait_ge(S.fino, NS)
    ve.wait_ge(S.parr, len(out))
    ve.tensor_tensor(T.osb[:, :], T.acco[:, 0:TK], T.pin[:, :], AluOpType.add).then_inc(S.ov, 1)
    g.sync.wait_ge(S.ov, 1)
    g.sync.dma_start(T.dx[:, :], T.osb[:, :]).then_inc(S.st, 16)
    g.sync.wait_ge(S.st, 16)
